import numpy as np
import ml_dtypes


def mxq(x, axis, fmt="e4m3"):
    dtype, down = {"e4m3": (ml_dtypes.float8_e4m3fn, 7), "e5m2": (ml_dtypes.float8_e5m2, 14)}[fmt]
    v = np.moveaxis(np.asarray(x, np.float32).astype(ml_dtypes.bfloat16).astype(np.float64), axis, -1)
    blocks = v.reshape(v.shape[:-1] + (-1, 32))
    amax = np.abs(blocks).max(-1, keepdims=True)
    byte = np.maximum(np.where(amax > 0, np.frexp(amax)[1] - 1 + 127, 0) - down, 1)
    scale = np.exp2(byte - 127.0)
    codes = (blocks / scale).astype(np.float32).astype(dtype).astype(np.float64)
    return np.moveaxis((codes * scale).reshape(v.shape), -1, axis)


WIDE = False


def mx_kscale(k):
    if not WIDE:
        return np.ones(k)
    levels = np.array([10, -10, 5, -5, 0])
    if k % 512:
        return np.exp2(np.random.permutation(np.resize(levels, k // 32))).repeat(32)
    a = np.empty((k // 512, 16))
    for p in range(k // 512):
        a[p, :8] = np.random.permutation(np.resize(levels, 8))
        for g in range(8):
            far = levels[np.abs(levels - a[p, g]) >= 10]
            a[p, g + 8] = far[np.random.randint(len(far))]
    return np.exp2(a.ravel()).repeat(32)


def f64(x):
    return np.asarray(x).astype(np.float64)


def striped(idx):
    return np.tile(idx.reshape(-1, 16).T, (8, 1)).astype(np.uint16)


def unstriped(offs):
    return offs[:16].T.reshape(-1).astype(np.int64)


E2M1 = np.array([0.0, 0.5, 1.0, 1.5, 2.0, 3.0, 4.0, 6.0, -0.0, -0.5, -1.0, -1.5, -2.0, -3.0, -4.0, -6.0])


def pack_weight(w, fmt):
    k, n = w.shape
    w = f64(np.asarray(w, np.float32).astype(ml_dtypes.bfloat16)).reshape(k // 32, 32, n)
    amax = np.abs(w).max(1)
    if fmt == "e4m3":
        byte = np.frexp(amax)[1] - 1 + 127 - 7
    else:
        mant, ex = np.frexp(amax / 6.0)
        byte = np.where(mant > 0.5, ex, ex - 1) + 127
    byte = np.clip(np.where(amax > 0, byte, 1), 1, 254)
    scaled = (w * np.exp2(127.0 - byte)[:, None, :]).reshape(k, n).astype(np.float32)
    by_word = np.ascontiguousarray(scaled.reshape(k // 512, 128, 4, n).transpose(0, 1, 3, 2))
    if fmt == "e4m3":
        words = by_word.astype(ml_dtypes.float8_e4m3fn).view(np.uint8)
    else:
        c = by_word.astype(ml_dtypes.float4_e2m1fn).view(np.uint8) & 0xF
        words = (c[..., 0::2] | (c[..., 1::2] << 4)).reshape(k // 512, 128, 2 * n)
    return np.ascontiguousarray(words), np.ascontiguousarray(byte.astype(np.uint8).reshape(k // 512, 16, n))


def unpack_weight(words, scales, fmt):
    g, _, n = scales.shape
    words = np.ascontiguousarray(words).reshape(g, 128, n, -1)
    if fmt == "e4m3":
        vals = words.view(ml_dtypes.float8_e4m3fn).astype(np.float64)
    else:
        nib = np.empty((g, 128, n, 4), np.uint8)
        nib[..., 0::2] = words & 0xF
        nib[..., 1::2] = words >> 4
        vals = E2M1[nib]
    vals = vals * np.repeat(np.exp2(scales.astype(np.float64) - 127.0), 8, axis=1)[..., None]
    return vals.transpose(0, 1, 3, 2).reshape(g * 512, n)


def gelu(v):
    return 0.5 * v * (1.0 + np.tanh(np.sqrt(2.0 / np.pi) * (v + 0.044715 * v**3)))


def striped8(idx):
    return np.concatenate([v.reshape(-1, 16).T for v in idx]).astype(np.uint16)


def unstriped8(offs):
    return np.stack([offs[16 * g:16 * g + 16].T.reshape(-1) for g in range(8)]).astype(np.int64)


def put_heads(h, wgs, idx8, t2):
    r = np.arange(h.shape[0])
    page = np.zeros((h.shape[0], t2))
    page[r[:, None], idx8[r % 512 // 64]] = wgs[r // 4 % 128] * h
    return page


K, T, S, H, T2, P = 1536, 2048, 512, 1024, 1024, 512


def setup_inputs():
    n = np.random.standard_normal
    s = mx_kscale(K)[:, None]
    u = mx_kscale(H)[:, None]
    tab_words, tab_scales = pack_weight(n((K, T)) * s, "e4m3")
    w4_words, w4_scales = pack_weight(n((K, H)) / np.sqrt(K) / s, "e2m1")
    slots = np.stack([np.random.permutation(T2)[:S] for _ in range(8)])
    return {
        "tab_words": tab_words,
        "tab_scales": tab_scales,
        "offs": striped(np.random.permutation(T)[:S]),
        "w4_words": w4_words,
        "w4_scales": w4_scales,
        "base": (0.8 * n((H, S))).astype(np.float32),
        "gain": (1.5 * np.exp(0.3 * n(H))).astype(np.float32),
        "wgs": np.repeat(np.random.uniform(0.5, 2.0, (8, S)), 16, axis=0).astype(np.float32),
        "offs2": striped8(slots),
        "offs3": striped(np.random.permutation(T2)[:P]),
        "gmap": (n((H, P)) * u).astype(np.float32),
        "w2": (1.5 * n((H, H)) / np.sqrt(H) / u).astype(np.float32),
    }


def reference(tab_words, tab_scales, offs, w4_words, w4_scales, base, gain, wgs, offs2, offs3, gmap, w2):
    v = unpack_weight(tab_words, tab_scales, "e4m3")[:, unstriped(offs)]
    w4 = unpack_weight(w4_words, w4_scales, "e2m1")
    h = f64(gain)[:, None] * np.tanh((w4.T @ v) + f64(base))
    page = put_heads(h, f64(wgs), unstriped8(offs2), T2)
    x = page[:, unstriped(offs3)]
    z = mxq(f64(gmap) * np.exp(np.tanh(x)), 0, "e4m3")
    w2q = mxq(f64(w2), 0, "e4m3")
    return (w2q.T @ z) + x

@@ -1,0 +1,214 @@
+from contextlib import ExitStack
+
+import concourse.mybir as mybir
+
+K, T, S, H, T2, M = 1536, 2048, 512, 1024, 1024, 512
+FLOPS = 2 * K * H * S + 2 * H * H * M
+
+F32 = mybir.dt.float32
+BF16 = mybir.dt.bfloat16
+I32 = mybir.dt.int32
+U32 = mybir.dt.uint32
+U16 = mybir.dt.uint16
+U8 = mybir.dt.uint8
+FP8X4 = mybir.dt.float8_e4m3fn_x4
+FP4X4 = mybir.dt.float4_e2m1fn_x4
+ALU = mybir.AluOpType
+ACT = mybir.ActivationFunctionType
+
+P = 128
+PACK = 4
+KPASS = P * PACK
+PASSES1 = K // KPASS
+PASSES2 = H // KPASS
+SLICES = H // P
+HALF = M // 2
+PAGES = 2
+
+
+def tile_list_flyover_source_map_kernel(
+    tc, tab_words, tab_scales, offs, w4_words, w4_scales, base, gain, wgs, offs2, offs3, gmap, w2, out
+):
+    nc = tc.nc
+    with ExitStack() as ctx:
+        lists = ctx.enter_context(tc.tile_pool(name="lists", bufs=1))
+        keep = ctx.enter_context(tc.tile_pool(name="keep", bufs=1))
+        ring = ctx.enter_context(tc.tile_pool(name="ring", bufs=2))
+        psum = ctx.enter_context(tc.psum_pool(name="psum", bufs=1))
+
+        def by_rows(ap):
+            return ap.rearrange("(b p i) c -> b p i c", p=P, i=PACK)
+
+        tab_s = keep.tile([P, PASSES1, T], U8, name="tab_s", tag="stage2")
+        w4_s = keep.tile([P, PASSES1, H], U8, name="w4_s", tag="stage4")
+        nc.vector.memset(tab_s[:].bitcast(I32), 0)
+        nc.vector.memset(w4_s[:].bitcast(I32), 0)
+        pages = [keep.tile([P, T2], F32, name=f"page{g}") for g in range(PAGES)]
+        for page in pages:
+            nc.vector.memset(page[:], 0.0)
+
+        idx1 = lists.tile([P, S // 16], U16, name="idx1")
+        idx2 = lists.tile([P, S // 16], U16, name="idx2")
+        idx3 = lists.tile([P, M // 16], U16, name="idx3")
+        gain_t = keep.tile([P, PASSES2, PACK], F32, name="gain_t")
+        wgs_t = keep.tile([P, S], F32, name="wgs_t", tag="stage5")
+
+        w2_parts = [(a, b) for a in range(PASSES2) for b in range(PASSES2)]
+
+        def load_tab(a):
+            words = keep.tile([P, T], I32, name=f"tab_w{a}", tag=f"stage{a % 2}")
+            nc.sync.dma_start(words[:], tab_words[a].rearrange("p t i -> p (t i)").bitcast(I32))
+            return words
+
+        def load_rows(name, src, tag):
+            rows = keep.tile([P, PACK, KPASS], F32, name=name, tag=tag)
+            nc.sync.dma_start(rows[:], src)
+            return rows
+
+        def load_scales(plane, scales):
+            for q in (0, 2, 1, 3):
+                nc.scalar.dma_start(
+                    plane[32 * q : 32 * q + 4].bitcast(I32),
+                    scales[:, 4 * q : 4 * q + 4, :].rearrange("a r t -> r a t").bitcast(I32),
+                )
+
+        nc.gpsimd.dma_start(gain_t[:], gain.rearrange("(b p i) -> p b i", p=P, i=PACK))
+        nc.gpsimd.dma_start(wgs_t[:], wgs)
+        nc.sync.dma_start(idx1[:], offs)
+        nc.sync.dma_start(idx2[:], offs2)
+        nc.sync.dma_start(idx3[:], offs3)
+        tab_w = [load_tab(0), load_tab(1)]
+        w4_w = keep.tile([P, PASSES1, 2 * H], U8, name="w4_w", tag="stage3")
+        nc.sync.dma_start(w4_w[:].bitcast(I32), w4_words.rearrange("a p c -> p a c").bitcast(I32))
+        load_scales(tab_s, tab_scales)
+        load_scales(w4_s, w4_scales)
+
+        wg = keep.tile([P, SLICES, S], F32, name="wg")
+        for s in range(SLICES):
+            b, i = divmod(s, PACK)
+            nc.scalar.activation(wg[:, s, :], wgs_t[:], ACT.Copy, scale=gain_t[:, b, i : i + 1])
+
+        v_w = [keep.tile([P, S], U32, name=f"v_w{a}", align_bytes=64) for a in range(PASSES1)]
+        v_s = [keep.tile([P, S], U8, name=f"v_s{a}", align_bytes=64) for a in range(PASSES1)]
+        w4p_w = [keep.tile([P, PASSES1, 2 * KPASS], U8, name=f"w4p_w{b}", align_bytes=64) for b in range(PASSES2)]
+        w4p_s = [keep.tile([P, PASSES1, KPASS], U8, name=f"w4p_s{b}", align_bytes=64) for b in range(PASSES2)]
+
+        def deal_w4(b):
+            nc.vector.tensor_copy(
+                w4p_w[b][:].bitcast(U16).rearrange("p a (i q) -> p a i q", i=PACK),
+                w4_w[:].bitcast(U16)[:, :, KPASS * b : KPASS * (b + 1)].rearrange("p a (q i) -> p a i q", i=PACK),
+            )
+            nc.vector.tensor_copy(
+                w4p_s[b][:].rearrange("p a (i q) -> p a i q", i=PACK),
+                w4_s[:, :, KPASS * b : KPASS * (b + 1)].rearrange("p a (q i) -> p a i q", i=PACK),
+            )
+
+        def pick_words(a):
+            nc.vector.tensor_copy(v_w[a][:], tab_w[a][:].bitcast(U32).indirect(idx1[:]))
+
+        pick_words(0)
+        tab_w.append(load_tab(2))
+        pick_words(1)
+        base0 = keep.tile([P, PACK, S], F32, name="base0", tag="stage1")
+        nc.sync.dma_start(base0[:, 0:1, :], by_rows(base)[0][:, 0:1, :])
+        nc.sync.dma_start(base0[:, 1:PACK, :], by_rows(base)[0][:, 1:PACK, :])
+        pick_words(2)
+        base_t = [base0, load_rows("base1", by_rows(base)[1], "stage5")]
+        for a in range(PASSES1):
+            nc.vector.tensor_copy(v_s[a][:], tab_s[:, a, :].indirect(idx1[:]))
+        deal_w4(0)
+
+        h = keep.tile([P, SLICES, S], F32, name="h")
+        for s in range(SLICES):
+            b, i = divmod(s, PACK)
+            if s == PACK:
+                deal_w4(1)
+            acc = psum.tile([P, S], F32, name=f"acc{s}", tag=f"bank{s}")
+            for a in range(PASSES1):
+                nc.tensor.matmul_mx(
+                    acc[:],
+                    lhsT=w4p_w[b][:, a, 2 * P * i : 2 * P * (i + 1)].bitcast(FP4X4),
+                    lhsT_scale=w4p_s[b][:, a, P * i : P * (i + 1)],
+                    rhs=v_w[a][:].bitcast(FP8X4),
+                    rhs_scale=v_s[a][:],
+                    start=(a == 0),
+                    stop=(a == PASSES1 - 1),
+                )
+            nc.vector.tensor_tensor(h[:, s, :], acc[:], base_t[b][:, i, :], ALU.add)
+            nc.scalar.activation(h[:, s, :], h[:, s, :], ACT.Tanh)
+
+        gmap_t = [load_rows("gmap0", by_rows(gmap)[0], "stage1"), load_rows("gmap1", by_rows(gmap)[1], "stage5")]
+        w2_stage = dict(zip(w2_parts, ("stage2", "stage0", "stage3", "stage4")))
+        w2_w, w2_s = {}, {}
+        for a, b in w2_parts:
+            raw = load_rows(f"w2raw{a}{b}", by_rows(w2)[a][:, :, KPASS * b : KPASS * (b + 1)], w2_stage[a, b])
+            rounded = ring.tile([P, PACK, P, PACK], BF16, name="rounded", align_bytes=64)
+            nc.scalar.copy(
+                rounded[:].rearrange("p i q j -> p q j i"),
+                raw[:].rearrange("p j (q i) -> p q j i", i=PACK),
+            )
+            w2_w[a, b] = keep.tile([P, KPASS], U32, name=f"w2_w{a}{b}", align_bytes=64)
+            w2_s[a, b] = keep.tile([P, KPASS], U8, name=f"w2_s{a}{b}", align_bytes=64)
+            nc.vector.quantize_mx(
+                w2_w[a, b][:].bitcast(FP8X4), w2_s[a, b][:], rounded[:].rearrange("p i q j -> p (i q j)")
+            )
+
+        halves = [slice(HALF * u, HALF * (u + 1)) for u in range(2)]
+        banks = {}
+        x_t = []
+        for b in range(PASSES2):
+            x = keep.tile([P, PACK, M], F32, name=f"x{b}", tag=("x0" if b == 0 else "stage1"))
+            e = keep.tile([P, PACK, M], F32, name=f"e{b}", tag=("stage4" if b == 0 else "stage0"))
+            x_t.append(x)
+
+            def put(i):
+                s = PACK * b + i
+                nc.vector.tensor_tensor(pages[s % PAGES][:].indirect(idx2[:]), h[:, s, :], wg[:, s, :], ALU.mult)
+
+            def fetch(i, cols):
+                s = PACK * b + i
+                picks = idx3[:, cols.start // 16 : cols.stop // 16]
+                nc.vector.tensor_copy(x[:, i, cols], pages[s % PAGES][:].indirect(picks))
+                nc.scalar.activation(e[:, i, cols], x[:, i, cols], ACT.Tanh)
+                nc.scalar.activation(e[:, i, cols], e[:, i, cols], ACT.Exp)
+
+            for i0 in range(0, PACK, PAGES):
+                last = b == PASSES2 - 1 and i0 == PACK - PAGES
+                for i in range(i0, i0 + PAGES):
+                    put(i)
+                for cols in halves if last else [slice(0, M)]:
+                    for i in range(i0, i0 + PAGES):
+                        fetch(i, cols)
+
+            for u, cols in enumerate(halves):
+                z = keep.tile([P, HALF, PACK], BF16, name=f"z{b}{u}", align_bytes=64)
+                nc.vector.tensor_tensor(
+                    z[:].rearrange("p (c n) i -> p c i n", n=2),
+                    e[:, :, cols].rearrange("p i (c n) -> p c i n", n=2),
+                    gmap_t[b][:, :, cols].rearrange("p i (c n) -> p c i n", n=2),
+                    ALU.mult,
+                )
+                z_w = keep.tile([P, HALF], U32, name=f"z_w{b}{u}", align_bytes=64)
+                z_s = keep.tile([P, HALF], U8, name=f"z_s{b}{u}", align_bytes=64)
+                nc.vector.quantize_mx(z_w[:].bitcast(FP8X4), z_s[:], z[:].rearrange("p c i -> p (c i)"))
+                for pair in range(SLICES // 2):
+                    if b == 0:
+                        banks[u, pair] = psum.tile([P, 2, HALF], F32, name=f"y{u}{pair}", tag=f"bank{4 * u + pair}")
+                    for j in range(2):
+                        nb, ni = divmod(2 * pair + j, PACK)
+                        nc.tensor.matmul_mx(
+                            banks[u, pair][:, j, :],
+                            lhsT=w2_w[b, nb][:, P * ni : P * (ni + 1)].bitcast(FP8X4),
+                            lhsT_scale=w2_s[b, nb][:, P * ni : P * (ni + 1)],
+                            rhs=z_w[:].bitcast(FP8X4),
+                            rhs_scale=z_s[:],
+                            start=(b == 0 and j == 0),
+                            stop=(b == PASSES2 - 1 and j == 1),
+                        )
+
+        for u, cols in enumerate(halves):
+            for pair in range(SLICES // 2):
+                nb, ni = divmod(2 * pair, PACK)
+                rows = x_t[nb][:, ni : ni + 2, cols]
+                nc.vector.tensor_tensor(rows, banks[u, pair][:], rows, ALU.add)
+                nc.sync.dma_start(by_rows(out)[nb][:, ni : ni + 2, cols], rows)

@@ -1,6 +1,7 @@
 from contextlib import ExitStack
 
 import concourse.mybir as mybir
+from concourse.masks import make_identity
 
 K, T, S, H, T2, M = 1536, 2048, 512, 1024, 1024, 512
 FLOPS = 2 * K * H * S + 2 * H * H * M
@@ -39,29 +40,34 @@ def tile_list_flyover_source_map_kernel(
         def by_rows(ap):
             return ap.rearrange("(b p i) c -> b p i c", p=P, i=PACK)
 
-        tab_s = keep.tile([P, PASSES1, T], U8, name="tab_s", tag="stage2")
-        w4_s = keep.tile([P, PASSES1, H], U8, name="w4_s", tag="stage4")
+        def stage(name, shape, dtype, slot):
+            return keep.tile(shape, dtype, name=name, tag=f"stage{slot}", align_bytes=64)
+
+        tab_s = stage("tab_s", [P, PASSES1, T], U8, 2)
+        w4_s = stage("w4_s", [P, PASSES1, H], U8, 4)
         nc.vector.memset(tab_s[:].bitcast(I32), 0)
         nc.vector.memset(w4_s[:].bitcast(I32), 0)
+        gain_t = keep.tile([P, PASSES2, PACK], F32, name="gain_t")
+        wgs_t = keep.tile([P, S], F32, name="wgs_t")
+        nc.gpsimd.dma_start(wgs_t[:], wgs)
+        nc.gpsimd.dma_start(gain_t[:], gain.rearrange("(b p i) -> p b i", p=P, i=PACK))
         pages = [keep.tile([P, T2], F32, name=f"page{g}") for g in range(PAGES)]
         for page in pages:
-            nc.vector.memset(page[:], 0.0)
+            nc.gpsimd.memset(page[:], 0.0)
+        ident = keep.tile([P, P], F32, name="ident")
+        make_identity(nc, ident[:])
 
         idx1 = lists.tile([P, S // 16], U16, name="idx1")
         idx2 = lists.tile([P, S // 16], U16, name="idx2")
         idx3 = lists.tile([P, M // 16], U16, name="idx3")
-        gain_t = keep.tile([P, PASSES2, PACK], F32, name="gain_t")
-        wgs_t = keep.tile([P, S], F32, name="wgs_t", tag="stage5")
-
-        w2_parts = [(a, b) for a in range(PASSES2) for b in range(PASSES2)]
 
         def load_tab(a):
-            words = keep.tile([P, T], I32, name=f"tab_w{a}", tag=f"stage{a % 2}")
+            words = stage(f"tab_w{a}", [P, T], I32, a % 2)
             nc.sync.dma_start(words[:], tab_words[a].rearrange("p t i -> p (t i)").bitcast(I32))
             return words
 
-        def load_rows(name, src, tag):
-            rows = keep.tile([P, PACK, KPASS], F32, name=name, tag=tag)
+        def load_rows(name, src, slot):
+            rows = stage(name, [P, PACK, KPASS], F32, slot)
             nc.sync.dma_start(rows[:], src)
             return rows
 
@@ -72,36 +78,28 @@ def tile_list_flyover_source_map_kernel(
                     scales[:, 4 * q : 4 * q + 4, :].rearrange("a r t -> r a t").bitcast(I32),
                 )
 
-        nc.gpsimd.dma_start(gain_t[:], gain.rearrange("(b p i) -> p b i", p=P, i=PACK))
-        nc.gpsimd.dma_start(wgs_t[:], wgs)
         nc.sync.dma_start(idx1[:], offs)
         nc.sync.dma_start(idx2[:], offs2)
         nc.sync.dma_start(idx3[:], offs3)
         tab_w = [load_tab(0), load_tab(1)]
-        w4_w = keep.tile([P, PASSES1, 2 * H], U8, name="w4_w", tag="stage3")
+        w4_w = stage("w4_w", [P, PASSES1, 2 * H], U8, 3)
         nc.sync.dma_start(w4_w[:].bitcast(I32), w4_words.rearrange("a p c -> p a c").bitcast(I32))
         load_scales(tab_s, tab_scales)
         load_scales(w4_s, w4_scales)
 
-        wg = keep.tile([P, SLICES, S], F32, name="wg")
-        for s in range(SLICES):
-            b, i = divmod(s, PACK)
-            nc.scalar.activation(wg[:, s, :], wgs_t[:], ACT.Copy, scale=gain_t[:, b, i : i + 1])
-
         v_w = [keep.tile([P, S], U32, name=f"v_w{a}", align_bytes=64) for a in range(PASSES1)]
         v_s = [keep.tile([P, S], U8, name=f"v_s{a}", align_bytes=64) for a in range(PASSES1)]
-        w4p_w = [keep.tile([P, PASSES1, 2 * KPASS], U8, name=f"w4p_w{b}", align_bytes=64) for b in range(PASSES2)]
-        w4p_s = [keep.tile([P, PASSES1, KPASS], U8, name=f"w4p_s{b}", align_bytes=64) for b in range(PASSES2)]
 
-        def deal_w4(b):
+        def deal_w4(b, dealt_w, dealt_s):
             nc.vector.tensor_copy(
-                w4p_w[b][:].bitcast(U16).rearrange("p a (i q) -> p a i q", i=PACK),
-                w4_w[:].bitcast(U16)[:, :, KPASS * b : KPASS * (b + 1)].rearrange("p a (q i) -> p a i q", i=PACK),
+                dealt_w[:].bitcast(U16).rearrange("p a (i q) -> p i a q", i=PACK),
+                w4_w[:].bitcast(U16)[:, :, KPASS * b : KPASS * (b + 1)].rearrange("p a (q i) -> p i a q", i=PACK),
             )
             nc.vector.tensor_copy(
-                w4p_s[b][:].rearrange("p a (i q) -> p a i q", i=PACK),
-                w4_s[:, :, KPASS * b : KPASS * (b + 1)].rearrange("p a (q i) -> p a i q", i=PACK),
+                dealt_s[:].rearrange("p a (i q) -> p i a q", i=PACK),
+                w4_s[:, :, KPASS * b : KPASS * (b + 1)].rearrange("p a (q i) -> p i a q", i=PACK),
             )
+            return dealt_w, dealt_s
 
         def pick_words(a):
             nc.vector.tensor_copy(v_w[a][:], tab_w[a][:].bitcast(U32).indirect(idx1[:]))
@@ -109,44 +107,70 @@ def tile_list_flyover_source_map_kernel(
         pick_words(0)
         tab_w.append(load_tab(2))
         pick_words(1)
-        base0 = keep.tile([P, PACK, S], F32, name="base0", tag="stage1")
-        nc.sync.dma_start(base0[:, 0:1, :], by_rows(base)[0][:, 0:1, :])
-        nc.sync.dma_start(base0[:, 1:PACK, :], by_rows(base)[0][:, 1:PACK, :])
+        base_first = stage("base_first", [P, S], F32, 1)
+        nc.sync.dma_start(base_first[:], by_rows(base)[0][:, 0, :])
         pick_words(2)
-        base_t = [base0, load_rows("base1", by_rows(base)[1], "stage5")]
         for a in range(PASSES1):
             nc.vector.tensor_copy(v_s[a][:], tab_s[:, a, :].indirect(idx1[:]))
-        deal_w4(0)
+        w4p_w0 = keep.tile([P, PASSES1, 2 * KPASS], U8, name="w4p_w0", align_bytes=64)
+        w4p_s0 = keep.tile([P, PASSES1, KPASS], U8, name="w4p_s0", align_bytes=64)
+        w4p = [deal_w4(0, w4p_w0, w4p_s0)]
+        base_rest = stage("base_rest", [P, PACK - 1, S], F32, 2)
+        nc.sync.dma_start(base_rest[:], by_rows(base)[0][:, 1:PACK, :])
+        base_rows = [base_first[:]] + [base_rest[:, i, :] for i in range(PACK - 1)]
 
         h = keep.tile([P, SLICES, S], F32, name="h")
+        wg0 = keep.tile([P, S], F32, name="wg0")
+        nc.scalar.activation(wg0[:], wgs_t[:], ACT.Copy, scale=gain_t[:, 0, 0:1])
+        blocks = [slice(P * j, P * (j + 1)) for j in range(S // P)]
         for s in range(SLICES):
             b, i = divmod(s, PACK)
             if s == PACK:
-                deal_w4(1)
-            acc = psum.tile([P, S], F32, name=f"acc{s}", tag=f"bank{s}")
+                w4p_w1 = stage("w4p_w1", [P, PASSES1, 2 * KPASS], U8, 1)
+                w4p.append(deal_w4(1, w4p_w1, stage("w4p_s1", [P, PASSES1, KPASS], U8, 0)))
+                base1 = load_rows("base1", by_rows(base)[1], 4)
+                base_rows.extend(base1[:, i, :] for i in range(PACK))
+            acc = psum.tile([P, S], F32, name=f"acc{s}", tag=f"bank{s % 3}")
             for a in range(PASSES1):
                 nc.tensor.matmul_mx(
                     acc[:],
-                    lhsT=w4p_w[b][:, a, 2 * P * i : 2 * P * (i + 1)].bitcast(FP4X4),
-                    lhsT_scale=w4p_s[b][:, a, P * i : P * (i + 1)],
+                    lhsT=w4p[b][0][:, a, 2 * P * i : 2 * P * (i + 1)].bitcast(FP4X4),
+                    lhsT_scale=w4p[b][1][:, a, P * i : P * (i + 1)],
                     rhs=v_w[a][:].bitcast(FP8X4),
                     rhs_scale=v_s[a][:],
                     start=(a == 0),
                     stop=(a == PASSES1 - 1),
                 )
-            nc.vector.tensor_tensor(h[:, s, :], acc[:], base_t[b][:, i, :], ALU.add)
-            nc.scalar.activation(h[:, s, :], h[:, s, :], ACT.Tanh)
+            if s == 0:
+                pre = keep.tile([P, S], F32, name="pre", tag="prod1")
+                nc.vector.tensor_tensor(pre[:], acc[:], base_rows[s], ALU.add)
+                nc.scalar.activation(h[:, s, :], pre[:], ACT.Tanh)
+                continue
+            prod = keep.tile([P, S], F32, name="prod", tag=f"prod{s % 2}")
+            nc.scalar.copy(prod[:], acc[:])
+            turned = psum.tile([P, S], F32, name=f"turned{s}", tag=f"bank{3 + s % 3}")
+            terms = [(prod[:], blk) for blk in blocks] + [(base_rows[s], blk) for blk in blocks]
+            for n, (term, blk) in enumerate(terms):
+                nc.tensor.matmul(
+                    turned[:, blk], term[:, blk], ident[:], start=(n == 0), stop=(n == len(terms) - 1), is_transpose=True
+                )
+            tanh_t = ring.tile([P, S], F32, name="tanh_t")
+            nc.scalar.activation(tanh_t[:], turned[:], ACT.Tanh)
+            back = psum.tile([P, S], F32, name=f"back{s}", tag=f"bank{6 + s % 2}")
+            for blk in blocks:
+                nc.tensor.transpose(back[:, blk], tanh_t[:, blk], ident[:])
+            nc.scalar.activation(h[:, s, :], back[:], ACT.Copy, scale=gain_t[:, b, i : i + 1])
 
-        gmap_t = [load_rows("gmap0", by_rows(gmap)[0], "stage1"), load_rows("gmap1", by_rows(gmap)[1], "stage5")]
-        w2_stage = dict(zip(w2_parts, ("stage2", "stage0", "stage3", "stage4")))
         w2_w, w2_s = {}, {}
-        for a, b in w2_parts:
-            raw = load_rows(f"w2raw{a}{b}", by_rows(w2)[a][:, :, KPASS * b : KPASS * (b + 1)], w2_stage[a, b])
+
+        def quantise_w2(a, b, slot):
+            raw = load_rows(f"w2raw{a}{b}", by_rows(w2)[a][:, :, KPASS * b : KPASS * (b + 1)], slot)
             rounded = ring.tile([P, PACK, P, PACK], BF16, name="rounded", align_bytes=64)
-            nc.scalar.copy(
-                rounded[:].rearrange("p i q j -> p q j i"),
-                raw[:].rearrange("p j (q i) -> p q j i", i=PACK),
-            )
+            for q0 in range(0, P, 32):
+                nc.scalar.copy(
+                    rounded[:].rearrange("p i q j -> p q j i")[:, q0 : q0 + 32],
+                    raw[:].rearrange("p j (q i) -> p q j i", i=PACK)[:, q0 : q0 + 32],
+                )
             w2_w[a, b] = keep.tile([P, KPASS], U32, name=f"w2_w{a}{b}", align_bytes=64)
             w2_s[a, b] = keep.tile([P, KPASS], U8, name=f"w2_s{a}{b}", align_bytes=64)
             nc.vector.quantize_mx(
@@ -157,13 +181,18 @@ def tile_list_flyover_source_map_kernel(
         banks = {}
         x_t = []
         for b in range(PASSES2):
-            x = keep.tile([P, PACK, M], F32, name=f"x{b}", tag=("x0" if b == 0 else "stage1"))
-            e = keep.tile([P, PACK, M], F32, name=f"e{b}", tag=("stage4" if b == 0 else "stage0"))
+            quantise_w2(b, 0, (2, 1)[b])
+            quantise_w2(b, 1, (3, 0)[b])
+            gmap_t = load_rows(f"gmap{b}", by_rows(gmap)[b], (4, 2)[b])
+            x = keep.tile([P, PACK, M], F32, name="x0") if b == 0 else stage("x1", [P, PACK, M], F32, 4)
+            e = stage(f"e{b}", [P, PACK, M], F32, (3, 0)[b])
+            z_rows = keep.tile([P, PACK, M], BF16, name=f"z_rows{b}")
             x_t.append(x)
 
             def put(i):
                 s = PACK * b + i
-                nc.vector.tensor_tensor(pages[s % PAGES][:].indirect(idx2[:]), h[:, s, :], wg[:, s, :], ALU.mult)
+                weight = wg0 if s == 0 else wgs_t
+                nc.vector.tensor_tensor(pages[s % PAGES][:].indirect(idx2[:]), h[:, s, :], weight[:], ALU.mult)
 
             def fetch(i, cols):
                 s = PACK * b + i
@@ -171,6 +200,7 @@ def tile_list_flyover_source_map_kernel(
                 nc.vector.tensor_copy(x[:, i, cols], pages[s % PAGES][:].indirect(picks))
                 nc.scalar.activation(e[:, i, cols], x[:, i, cols], ACT.Tanh)
                 nc.scalar.activation(e[:, i, cols], e[:, i, cols], ACT.Exp)
+                nc.vector.tensor_tensor(z_rows[:, i, cols], e[:, i, cols], gmap_t[:, i, cols], ALU.mult)
 
             for i0 in range(0, PACK, PAGES):
                 last = b == PASSES2 - 1 and i0 == PACK - PAGES
@@ -182,11 +212,10 @@ def tile_list_flyover_source_map_kernel(
 
             for u, cols in enumerate(halves):
                 z = keep.tile([P, HALF, PACK], BF16, name=f"z{b}{u}", align_bytes=64)
-                nc.vector.tensor_tensor(
-                    z[:].rearrange("p (c n) i -> p c i n", n=2),
-                    e[:, :, cols].rearrange("p i (c n) -> p c i n", n=2),
-                    gmap_t[b][:, :, cols].rearrange("p i (c n) -> p c i n", n=2),
-                    ALU.mult,
+                weave = nc.vector.tensor_copy if (b, u) == (PASSES2 - 1, 0) else nc.scalar.copy
+                weave(
+                    z[:].rearrange("p (c n) i -> p c i n", n=4),
+                    z_rows[:, :, cols].rearrange("p i (c n) -> p c i n", n=4),
                 )
                 z_w = keep.tile([P, HALF], U32, name=f"z_w{b}{u}", align_bytes=64)
                 z_s = keep.tile([P, HALF], U8, name=f"z_s{b}{u}", align_bytes=64)

@@ -49,13 +49,13 @@ def tile_list_flyover_source_map_kernel(
         nc.vector.memset(w4_s[:].bitcast(I32), 0)
         gain_t = keep.tile([P, PASSES2, PACK], F32, name="gain_t")
         wgs_t = keep.tile([P, S], F32, name="wgs_t")
-        nc.gpsimd.dma_start(wgs_t[:], wgs)
-        nc.gpsimd.dma_start(gain_t[:], gain.rearrange("(b p i) -> p b i", p=P, i=PACK))
         pages = [keep.tile([P, T2], F32, name=f"page{g}") for g in range(PAGES)]
         for page in pages:
             nc.gpsimd.memset(page[:], 0.0)
         ident = keep.tile([P, P], F32, name="ident")
         make_identity(nc, ident[:])
+        nc.gpsimd.dma_start(wgs_t[:], wgs)
+        nc.gpsimd.dma_start(gain_t[:], gain.rearrange("(b p i) -> p b i", p=P, i=PACK))
 
         idx1 = lists.tile([P, S // 16], U16, name="idx1")
         idx2 = lists.tile([P, S // 16], U16, name="idx2")
@@ -64,6 +64,12 @@ def tile_list_flyover_source_map_kernel(
         def load_tab(a):
             words = stage(f"tab_w{a}", [P, T], I32, a % 2)
             nc.sync.dma_start(words[:], tab_words[a].rearrange("p t i -> p (t i)").bitcast(I32))
+            return words
+
+        def load_w4(b):
+            words = stage(f"w4_w{b}", [P, PASSES1, 2 * KPASS], U8, 3)
+            cols = slice(2 * KPASS * b, 2 * KPASS * (b + 1))
+            nc.sync.dma_start(words[:].bitcast(I32), w4_words[:, :, cols].rearrange("a p c -> p a c").bitcast(I32))
             return words
 
         def load_rows(name, src, slot):
@@ -82,8 +88,7 @@ def tile_list_flyover_source_map_kernel(
         nc.sync.dma_start(idx2[:], offs2)
         nc.sync.dma_start(idx3[:], offs3)
         tab_w = [load_tab(0), load_tab(1)]
-        w4_w = stage("w4_w", [P, PASSES1, 2 * H], U8, 3)
-        nc.sync.dma_start(w4_w[:].bitcast(I32), w4_words.rearrange("a p c -> p a c").bitcast(I32))
+        w4_w = [load_w4(0)]
         load_scales(tab_s, tab_scales)
         load_scales(w4_s, w4_scales)
 
@@ -93,7 +98,7 @@ def tile_list_flyover_source_map_kernel(
         def deal_w4(b, dealt_w, dealt_s):
             nc.vector.tensor_copy(
                 dealt_w[:].bitcast(U16).rearrange("p a (i q) -> p i a q", i=PACK),
-                w4_w[:].bitcast(U16)[:, :, KPASS * b : KPASS * (b + 1)].rearrange("p a (q i) -> p i a q", i=PACK),
+                w4_w[b][:].bitcast(U16).rearrange("p a (q i) -> p i a q", i=PACK),
             )
             nc.vector.tensor_copy(
                 dealt_s[:].rearrange("p a (i q) -> p i a q", i=PACK),
@@ -115,6 +120,7 @@ def tile_list_flyover_source_map_kernel(
         w4p_w0 = keep.tile([P, PASSES1, 2 * KPASS], U8, name="w4p_w0", align_bytes=64)
         w4p_s0 = keep.tile([P, PASSES1, KPASS], U8, name="w4p_s0", align_bytes=64)
         w4p = [deal_w4(0, w4p_w0, w4p_s0)]
+        w4_w.append(load_w4(1))
         base_rest = stage("base_rest", [P, PACK - 1, S], F32, 2)
         nc.sync.dma_start(base_rest[:], by_rows(base)[0][:, 1:PACK, :])
         base_rows = [base_first[:]] + [base_rest[:, i, :] for i in range(PACK - 1)]
@@ -130,7 +136,7 @@ def tile_list_flyover_source_map_kernel(
                 w4p.append(deal_w4(1, w4p_w1, stage("w4p_s1", [P, PASSES1, KPASS], U8, 0)))
                 base1 = load_rows("base1", by_rows(base)[1], 4)
                 base_rows.extend(base1[:, i, :] for i in range(PACK))
-            acc = psum.tile([P, S], F32, name=f"acc{s}", tag=f"bank{s % 3}")
+            acc = psum.tile([P, S], F32, name=f"acc{s}", tag=f"bank{s % 2}")
             for a in range(PASSES1):
                 nc.tensor.matmul_mx(
                     acc[:],
@@ -142,13 +148,12 @@ def tile_list_flyover_source_map_kernel(
                     stop=(a == PASSES1 - 1),
                 )
             if s == 0:
-                pre = keep.tile([P, S], F32, name="pre", tag="prod1")
-                nc.vector.tensor_tensor(pre[:], acc[:], base_rows[s], ALU.add)
-                nc.scalar.activation(h[:, s, :], pre[:], ACT.Tanh)
+                nc.vector.tensor_tensor(h[:, s, :], acc[:], base_rows[s], ALU.add)
+                nc.scalar.activation(h[:, s, :], h[:, s, :], ACT.Tanh)
                 continue
-            prod = keep.tile([P, S], F32, name="prod", tag=f"prod{s % 2}")
+            prod = ring.tile([P, S], F32, name="prod")
             nc.scalar.copy(prod[:], acc[:])
-            turned = psum.tile([P, S], F32, name=f"turned{s}", tag=f"bank{3 + s % 3}")
+            turned = psum.tile([P, S], F32, name=f"turned{s}", tag=f"bank{2 + s % 3}")
             terms = [(prod[:], blk) for blk in blocks] + [(base_rows[s], blk) for blk in blocks]
             for n, (term, blk) in enumerate(terms):
                 nc.tensor.matmul(
@@ -156,10 +161,11 @@ def tile_list_flyover_source_map_kernel(
                 )
             tanh_t = ring.tile([P, S], F32, name="tanh_t")
             nc.scalar.activation(tanh_t[:], turned[:], ACT.Tanh)
-            back = psum.tile([P, S], F32, name=f"back{s}", tag=f"bank{6 + s % 2}")
+            back = psum.tile([P, S], F32, name=f"back{s}", tag=f"bank{5 + s % 3}")
             for blk in blocks:
                 nc.tensor.transpose(back[:, blk], tanh_t[:, blk], ident[:])
             nc.scalar.activation(h[:, s, :], back[:], ACT.Copy, scale=gain_t[:, b, i : i + 1])
+            nc.gpsimd.tensor_tensor(h[:, s, :], h[:, s, :], wgs_t[:], ALU.mult)
 
         w2_w, w2_s = {}, {}
 
@@ -191,8 +197,11 @@ def tile_list_flyover_source_map_kernel(
 
             def put(i):
                 s = PACK * b + i
-                weight = wg0 if s == 0 else wgs_t
-                nc.vector.tensor_tensor(pages[s % PAGES][:].indirect(idx2[:]), h[:, s, :], weight[:], ALU.mult)
+                places = pages[s % PAGES][:].indirect(idx2[:])
+                if s == 0:
+                    nc.vector.tensor_tensor(places, h[:, s, :], wg0[:], ALU.mult)
+                else:
+                    nc.vector.tensor_copy(places, h[:, s, :])
 
             def fetch(i, cols):
                 s = PACK * b + i
@@ -200,7 +209,8 @@ def tile_list_flyover_source_map_kernel(
                 nc.vector.tensor_copy(x[:, i, cols], pages[s % PAGES][:].indirect(picks))
                 nc.scalar.activation(e[:, i, cols], x[:, i, cols], ACT.Tanh)
                 nc.scalar.activation(e[:, i, cols], e[:, i, cols], ACT.Exp)
-                nc.vector.tensor_tensor(z_rows[:, i, cols], e[:, i, cols], gmap_t[:, i, cols], ALU.mult)
+                engine = nc.gpsimd if s < SLICES - PAGES else nc.vector
+                engine.tensor_tensor(z_rows[:, i, cols], e[:, i, cols], gmap_t[:, i, cols], ALU.mult)
 
             for i0 in range(0, PACK, PAGES):
                 last = b == PASSES2 - 1 and i0 == PACK - PAGES

@@ -25,6 +25,7 @@ PASSES2 = H // KPASS
 SLICES = H // P
 HALF = M // 2
 PAGES = 2
+DIRECT = 2
 
 
 def tile_list_flyover_source_map_kernel(
@@ -92,62 +93,61 @@ def tile_list_flyover_source_map_kernel(
         load_scales(tab_s, tab_scales)
         load_scales(w4_s, w4_scales)
 
-        v_w = [keep.tile([P, S], U32, name=f"v_w{a}", align_bytes=64) for a in range(PASSES1)]
-        v_s = [keep.tile([P, S], U8, name=f"v_s{a}", align_bytes=64) for a in range(PASSES1)]
+        def pick_words(words, picked):
+            nc.vector.tensor_copy(picked[:], words[:].bitcast(U32).indirect(idx1[:]))
+            return picked
 
-        def deal_w4(b, dealt_w, dealt_s):
+        def deal_words(words, dealt):
             nc.vector.tensor_copy(
-                dealt_w[:].bitcast(U16).rearrange("p a (i q) -> p i a q", i=PACK),
-                w4_w[b][:].bitcast(U16).rearrange("p a (q i) -> p i a q", i=PACK),
+                dealt[:].bitcast(U16).rearrange("p a (i q) -> p i a q", i=PACK),
+                words[:].bitcast(U16).rearrange("p a (q i) -> p i a q", i=PACK),
             )
-            nc.vector.tensor_copy(
-                dealt_s[:].rearrange("p a (i q) -> p i a q", i=PACK),
-                w4_s[:, :, KPASS * b : KPASS * (b + 1)].rearrange("p a (q i) -> p i a q", i=PACK),
-            )
-            return dealt_w, dealt_s
+            return dealt
 
-        def pick_words(a):
-            nc.vector.tensor_copy(v_w[a][:], tab_w[a][:].bitcast(U32).indirect(idx1[:]))
-
-        pick_words(0)
+        v_w = [pick_words(tab_w[0], keep.tile([P, S], U32, name="v_w0", align_bytes=64))]
         tab_w.append(load_tab(2))
-        pick_words(1)
-        base_first = stage("base_first", [P, S], F32, 1)
-        nc.sync.dma_start(base_first[:], by_rows(base)[0][:, 0, :])
-        pick_words(2)
+        v_w.append(pick_words(tab_w[1], keep.tile([P, S], U32, name="v_w1", align_bytes=64)))
+        base_first = stage("base_first", [P, DIRECT, S], F32, 1)
+        nc.sync.dma_start(base_first[:], by_rows(base)[0][:, 0:DIRECT, :])
+        v_s = [keep.tile([P, S], U8, name=f"v_s{a}", align_bytes=64) for a in range(PASSES1)]
         for a in range(PASSES1):
             nc.vector.tensor_copy(v_s[a][:], tab_s[:, a, :].indirect(idx1[:]))
-        w4p_w0 = keep.tile([P, PASSES1, 2 * KPASS], U8, name="w4p_w0", align_bytes=64)
-        w4p_s0 = keep.tile([P, PASSES1, KPASS], U8, name="w4p_s0", align_bytes=64)
-        w4p = [deal_w4(0, w4p_w0, w4p_s0)]
+        w4p_w = [deal_words(w4_w[0], keep.tile([P, PASSES1, 2 * KPASS], U8, name="w4p_w0", align_bytes=64))]
         w4_w.append(load_w4(1))
-        base_rest = stage("base_rest", [P, PACK - 1, S], F32, 2)
-        nc.sync.dma_start(base_rest[:], by_rows(base)[0][:, 1:PACK, :])
-        base_rows = [base_first[:]] + [base_rest[:, i, :] for i in range(PACK - 1)]
+        w4p_s = [keep.tile([P, PASSES1, KPASS], U8, name=f"w4p_s{b}", align_bytes=64) for b in range(PASSES2)]
+        for b in range(PASSES2):
+            nc.vector.tensor_copy(
+                w4p_s[b][:].rearrange("p a (i q) -> p i a q", i=PACK),
+                w4_s[:, :, KPASS * b : KPASS * (b + 1)].rearrange("p a (q i) -> p i a q", i=PACK),
+            )
+        v_w.append(pick_words(tab_w[2], stage("v_w2", [P, S], U32, 4)))
+        base_rest = stage("base_rest", [P, PACK - DIRECT, S], F32, 2)
+        nc.sync.dma_start(base_rest[:], by_rows(base)[0][:, DIRECT:PACK, :])
+        base_rows = [base_first[:, i, :] for i in range(DIRECT)] + [base_rest[:, i, :] for i in range(PACK - DIRECT)]
 
         h = keep.tile([P, SLICES, S], F32, name="h")
-        wg0 = keep.tile([P, S], F32, name="wg0")
-        nc.scalar.activation(wg0[:], wgs_t[:], ACT.Copy, scale=gain_t[:, 0, 0:1])
+        wg = keep.tile([P, DIRECT, S], F32, name="wg")
+        for s in range(DIRECT):
+            nc.scalar.activation(wg[:, s, :], wgs_t[:], ACT.Copy, scale=gain_t[:, 0, s : s + 1])
         blocks = [slice(P * j, P * (j + 1)) for j in range(S // P)]
         for s in range(SLICES):
             b, i = divmod(s, PACK)
             if s == PACK:
-                w4p_w1 = stage("w4p_w1", [P, PASSES1, 2 * KPASS], U8, 1)
-                w4p.append(deal_w4(1, w4p_w1, stage("w4p_s1", [P, PASSES1, KPASS], U8, 0)))
-                base1 = load_rows("base1", by_rows(base)[1], 4)
+                w4p_w.append(deal_words(w4_w[1], stage("w4p_w1", [P, PASSES1, 2 * KPASS], U8, 1)))
+                base1 = load_rows("base1", by_rows(base)[1], 0)
                 base_rows.extend(base1[:, i, :] for i in range(PACK))
             acc = psum.tile([P, S], F32, name=f"acc{s}", tag=f"bank{s % 2}")
             for a in range(PASSES1):
                 nc.tensor.matmul_mx(
                     acc[:],
-                    lhsT=w4p[b][0][:, a, 2 * P * i : 2 * P * (i + 1)].bitcast(FP4X4),
-                    lhsT_scale=w4p[b][1][:, a, P * i : P * (i + 1)],
+                    lhsT=w4p_w[b][:, a, 2 * P * i : 2 * P * (i + 1)].bitcast(FP4X4),
+                    lhsT_scale=w4p_s[b][:, a, P * i : P * (i + 1)],
                     rhs=v_w[a][:].bitcast(FP8X4),
                     rhs_scale=v_s[a][:],
                     start=(a == 0),
                     stop=(a == PASSES1 - 1),
                 )
-            if s == 0:
+            if s < DIRECT:
                 nc.vector.tensor_tensor(h[:, s, :], acc[:], base_rows[s], ALU.add)
                 nc.scalar.activation(h[:, s, :], h[:, s, :], ACT.Tanh)
                 continue
@@ -165,7 +165,6 @@ def tile_list_flyover_source_map_kernel(
             for blk in blocks:
                 nc.tensor.transpose(back[:, blk], tanh_t[:, blk], ident[:])
             nc.scalar.activation(h[:, s, :], back[:], ACT.Copy, scale=gain_t[:, b, i : i + 1])
-            nc.gpsimd.tensor_tensor(h[:, s, :], h[:, s, :], wgs_t[:], ALU.mult)
 
         w2_w, w2_s = {}, {}
 
@@ -187,21 +186,17 @@ def tile_list_flyover_source_map_kernel(
         banks = {}
         x_t = []
         for b in range(PASSES2):
-            quantise_w2(b, 0, (2, 1)[b])
-            quantise_w2(b, 1, (3, 0)[b])
-            gmap_t = load_rows(f"gmap{b}", by_rows(gmap)[b], (4, 2)[b])
-            x = keep.tile([P, PACK, M], F32, name="x0") if b == 0 else stage("x1", [P, PACK, M], F32, 4)
-            e = stage(f"e{b}", [P, PACK, M], F32, (3, 0)[b])
-            z_rows = keep.tile([P, PACK, M], BF16, name=f"z_rows{b}")
+            quantise_w2(b, 0, (2, 4)[b])
+            quantise_w2(b, 1, (3, 1)[b])
+            gmap_t = load_rows(f"gmap{b}", by_rows(gmap)[b], (3, 2)[b])
+            x = keep.tile([P, PACK, M], F32, name="x0") if b == 0 else stage("x1", [P, PACK, M], F32, 3)
+            e = stage(f"e{b}", [P, PACK, M], F32, b)
             x_t.append(x)
 
             def put(i):
                 s = PACK * b + i
-                places = pages[s % PAGES][:].indirect(idx2[:])
-                if s == 0:
-                    nc.vector.tensor_tensor(places, h[:, s, :], wg0[:], ALU.mult)
-                else:
-                    nc.vector.tensor_copy(places, h[:, s, :])
+                weight = wg[:, s, :] if s < DIRECT else wgs_t[:]
+                nc.vector.tensor_tensor(pages[s % PAGES][:].indirect(idx2[:]), h[:, s, :], weight, ALU.mult)
 
             def fetch(i, cols):
                 s = PACK * b + i
@@ -209,8 +204,6 @@ def tile_list_flyover_source_map_kernel(
                 nc.vector.tensor_copy(x[:, i, cols], pages[s % PAGES][:].indirect(picks))
                 nc.scalar.activation(e[:, i, cols], x[:, i, cols], ACT.Tanh)
                 nc.scalar.activation(e[:, i, cols], e[:, i, cols], ACT.Exp)
-                engine = nc.gpsimd if s < SLICES - PAGES else nc.vector
-                engine.tensor_tensor(z_rows[:, i, cols], e[:, i, cols], gmap_t[:, i, cols], ALU.mult)
 
             for i0 in range(0, PACK, PAGES):
                 last = b == PASSES2 - 1 and i0 == PACK - PAGES
@@ -222,10 +215,11 @@ def tile_list_flyover_source_map_kernel(
 
             for u, cols in enumerate(halves):
                 z = keep.tile([P, HALF, PACK], BF16, name=f"z{b}{u}", align_bytes=64)
-                weave = nc.vector.tensor_copy if (b, u) == (PASSES2 - 1, 0) else nc.scalar.copy
-                weave(
-                    z[:].rearrange("p (c n) i -> p c i n", n=4),
-                    z_rows[:, :, cols].rearrange("p i (c n) -> p c i n", n=4),
+                nc.vector.tensor_tensor(
+                    z[:].rearrange("p (c n) i -> p c i n", n=2),
+                    e[:, :, cols].rearrange("p i (c n) -> p c i n", n=2),
+                    gmap_t[:, :, cols].rearrange("p i (c n) -> p c i n", n=2),
+                    ALU.mult,
                 )
                 z_w = keep.tile([P, HALF], U32, name=f"z_w{b}{u}", align_bytes=64)
                 z_s = keep.tile([P, HALF], U8, name=f"z_s{b}{u}", align_bytes=64)

from contextlib import ExitStack

import concourse.mybir as mybir
from concourse.masks import make_identity

K, T, S, H, T2, M = 1536, 2048, 512, 1024, 1024, 512
FLOPS = 2 * K * H * S + 2 * H * H * M

F32 = mybir.dt.float32
BF16 = mybir.dt.bfloat16
I32 = mybir.dt.int32
U32 = mybir.dt.uint32
U16 = mybir.dt.uint16
U8 = mybir.dt.uint8
FP8X4 = mybir.dt.float8_e4m3fn_x4
FP4X4 = mybir.dt.float4_e2m1fn_x4
ALU = mybir.AluOpType
ACT = mybir.ActivationFunctionType

P = 128
PACK = 4
KPASS = P * PACK
PASSES1 = K // KPASS
PASSES2 = H // KPASS
SLICES = H // P
HALF = M // 2
PAGES = 2
DIRECT = 2


def tile_list_flyover_source_map_kernel(
    tc, tab_words, tab_scales, offs, w4_words, w4_scales, base, gain, wgs, offs2, offs3, gmap, w2, out
):
    nc = tc.nc
    with ExitStack() as ctx:
        lists = ctx.enter_context(tc.tile_pool(name="lists", bufs=1))
        keep = ctx.enter_context(tc.tile_pool(name="keep", bufs=1))
        ring = ctx.enter_context(tc.tile_pool(name="ring", bufs=2))
        psum = ctx.enter_context(tc.psum_pool(name="psum", bufs=1))

        def by_rows(ap):
            return ap.rearrange("(b p i) c -> b p i c", p=P, i=PACK)

        def stage(name, shape, dtype, slot):
            return keep.tile(shape, dtype, name=name, tag=f"stage{slot}", align_bytes=64)

        tab_s = stage("tab_s", [P, PASSES1, T], U8, 2)
        w4_s = stage("w4_s", [P, PASSES1, H], U8, 4)
        nc.vector.memset(tab_s[:].bitcast(I32), 0)
        nc.vector.memset(w4_s[:].bitcast(I32), 0)
        gain_t = keep.tile([P, PASSES2, PACK], F32, name="gain_t")
        wgs_t = keep.tile([P, S], F32, name="wgs_t")
        pages = [keep.tile([P, T2], F32, name=f"page{g}") for g in range(PAGES)]
        for page in pages:
            nc.gpsimd.memset(page[:], 0.0)
        ident = keep.tile([P, P], F32, name="ident")
        make_identity(nc, ident[:])
        nc.gpsimd.dma_start(wgs_t[:], wgs)
        nc.gpsimd.dma_start(gain_t[:], gain.rearrange("(b p i) -> p b i", p=P, i=PACK))

        idx1 = lists.tile([P, S // 16], U16, name="idx1")
        idx2 = lists.tile([P, S // 16], U16, name="idx2")
        idx3 = lists.tile([P, M // 16], U16, name="idx3")

        def load_tab(a):
            words = stage(f"tab_w{a}", [P, T], I32, a % 2)
            nc.sync.dma_start(words[:], tab_words[a].rearrange("p t i -> p (t i)").bitcast(I32))
            return words

        def load_w4(b):
            words = stage(f"w4_w{b}", [P, PASSES1, 2 * KPASS], U8, 3)
            cols = slice(2 * KPASS * b, 2 * KPASS * (b + 1))
            nc.sync.dma_start(words[:].bitcast(I32), w4_words[:, :, cols].rearrange("a p c -> p a c").bitcast(I32))
            return words

        def load_rows(name, src, slot):
            rows = stage(name, [P, PACK, KPASS], F32, slot)
            nc.sync.dma_start(rows[:], src)
            return rows

        def load_scales(plane, scales):
            for q in (0, 2, 1, 3):
                nc.scalar.dma_start(
                    plane[32 * q : 32 * q + 4].bitcast(I32),
                    scales[:, 4 * q : 4 * q + 4, :].rearrange("a r t -> r a t").bitcast(I32),
                )

        nc.sync.dma_start(idx1[:], offs)
        nc.sync.dma_start(idx2[:], offs2)
        nc.sync.dma_start(idx3[:], offs3)
        tab_w = [load_tab(0), load_tab(1)]
        w4_w = [load_w4(0)]
        load_scales(tab_s, tab_scales)
        load_scales(w4_s, w4_scales)

        def pick_words(words, picked):
            nc.vector.tensor_copy(picked[:], words[:].bitcast(U32).indirect(idx1[:]))
            return picked

        def deal_words(words, dealt):
            nc.vector.tensor_copy(
                dealt[:].bitcast(U16).rearrange("p a (i q) -> p i a q", i=PACK),
                words[:].bitcast(U16).rearrange("p a (q i) -> p i a q", i=PACK),
            )
            return dealt

        v_w = [pick_words(tab_w[0], keep.tile([P, S], U32, name="v_w0", align_bytes=64))]
        tab_w.append(load_tab(2))
        v_w.append(pick_words(tab_w[1], keep.tile([P, S], U32, name="v_w1", align_bytes=64)))
        base_first = stage("base_first", [P, DIRECT, S], F32, 1)
        nc.sync.dma_start(base_first[:], by_rows(base)[0][:, 0:DIRECT, :])
        v_s = [keep.tile([P, S], U8, name=f"v_s{a}", align_bytes=64) for a in range(PASSES1)]
        for a in range(PASSES1):
            nc.vector.tensor_copy(v_s[a][:], tab_s[:, a, :].indirect(idx1[:]))
        w4p_w = [deal_words(w4_w[0], keep.tile([P, PASSES1, 2 * KPASS], U8, name="w4p_w0", align_bytes=64))]
        w4_w.append(load_w4(1))
        w4p_s = [keep.tile([P, PASSES1, KPASS], U8, name=f"w4p_s{b}", align_bytes=64) for b in range(PASSES2)]
        for b in range(PASSES2):
            nc.vector.tensor_copy(
                w4p_s[b][:].rearrange("p a (i q) -> p i a q", i=PACK),
                w4_s[:, :, KPASS * b : KPASS * (b + 1)].rearrange("p a (q i) -> p i a q", i=PACK),
            )
        v_w.append(pick_words(tab_w[2], stage("v_w2", [P, S], U32, 4)))
        base_rest = stage("base_rest", [P, PACK - DIRECT, S], F32, 2)
        nc.sync.dma_start(base_rest[:], by_rows(base)[0][:, DIRECT:PACK, :])
        base_rows = [base_first[:, i, :] for i in range(DIRECT)] + [base_rest[:, i, :] for i in range(PACK - DIRECT)]

        h = keep.tile([P, SLICES, S], F32, name="h")
        wg = keep.tile([P, DIRECT, S], F32, name="wg")
        for s in range(DIRECT):
            nc.scalar.activation(wg[:, s, :], wgs_t[:], ACT.Copy, scale=gain_t[:, 0, s : s + 1])
        blocks = [slice(P * j, P * (j + 1)) for j in range(S // P)]
        for s in range(SLICES):
            b, i = divmod(s, PACK)
            if s == PACK:
                w4p_w.append(deal_words(w4_w[1], stage("w4p_w1", [P, PASSES1, 2 * KPASS], U8, 1)))
                base1 = load_rows("base1", by_rows(base)[1], 0)
                base_rows.extend(base1[:, i, :] for i in range(PACK))
            acc = psum.tile([P, S], F32, name=f"acc{s}", tag=f"bank{s % 2}")
            for a in range(PASSES1):
                nc.tensor.matmul_mx(
                    acc[:],
                    lhsT=w4p_w[b][:, a, 2 * P * i : 2 * P * (i + 1)].bitcast(FP4X4),
                    lhsT_scale=w4p_s[b][:, a, P * i : P * (i + 1)],
                    rhs=v_w[a][:].bitcast(FP8X4),
                    rhs_scale=v_s[a][:],
                    start=(a == 0),
                    stop=(a == PASSES1 - 1),
                )
            if s < DIRECT:
                nc.vector.tensor_tensor(h[:, s, :], acc[:], base_rows[s], ALU.add)
                nc.scalar.activation(h[:, s, :], h[:, s, :], ACT.Tanh)
                continue
            prod = ring.tile([P, S], F32, name="prod")
            nc.scalar.copy(prod[:], acc[:])
            turned = psum.tile([P, S], F32, name=f"turned{s}", tag=f"bank{2 + s % 3}")
            terms = [(prod[:], blk) for blk in blocks] + [(base_rows[s], blk) for blk in blocks]
            for n, (term, blk) in enumerate(terms):
                nc.tensor.matmul(
                    turned[:, blk], term[:, blk], ident[:], start=(n == 0), stop=(n == len(terms) - 1), is_transpose=True
                )
            tanh_t = ring.tile([P, S], F32, name="tanh_t")
            nc.scalar.activation(tanh_t[:], turned[:], ACT.Tanh)
            back = psum.tile([P, S], F32, name=f"back{s}", tag=f"bank{5 + s % 3}")
            for blk in blocks:
                nc.tensor.transpose(back[:, blk], tanh_t[:, blk], ident[:])
            nc.scalar.activation(h[:, s, :], back[:], ACT.Copy, scale=gain_t[:, b, i : i + 1])

        w2_w, w2_s = {}, {}

        def quantise_w2(a, b, slot):
            raw = load_rows(f"w2raw{a}{b}", by_rows(w2)[a][:, :, KPASS * b : KPASS * (b + 1)], slot)
            rounded = ring.tile([P, PACK, P, PACK], BF16, name="rounded", align_bytes=64)
            for q0 in range(0, P, 32):
                nc.scalar.copy(
                    rounded[:].rearrange("p i q j -> p q j i")[:, q0 : q0 + 32],
                    raw[:].rearrange("p j (q i) -> p q j i", i=PACK)[:, q0 : q0 + 32],
                )
            w2_w[a, b] = keep.tile([P, KPASS], U32, name=f"w2_w{a}{b}", align_bytes=64)
            w2_s[a, b] = keep.tile([P, KPASS], U8, name=f"w2_s{a}{b}", align_bytes=64)
            nc.vector.quantize_mx(
                w2_w[a, b][:].bitcast(FP8X4), w2_s[a, b][:], rounded[:].rearrange("p i q j -> p (i q j)")
            )

        halves = [slice(HALF * u, HALF * (u + 1)) for u in range(2)]
        banks = {}
        x_t = []
        for b in range(PASSES2):
            quantise_w2(b, 0, (2, 4)[b])
            quantise_w2(b, 1, (3, 1)[b])
            gmap_t = load_rows(f"gmap{b}", by_rows(gmap)[b], (3, 2)[b])
            x = keep.tile([P, PACK, M], F32, name="x0") if b == 0 else stage("x1", [P, PACK, M], F32, 3)
            e = stage(f"e{b}", [P, PACK, M], F32, b)
            x_t.append(x)

            def put(i):
                s = PACK * b + i
                weight = wg[:, s, :] if s < DIRECT else wgs_t[:]
                nc.vector.tensor_tensor(pages[s % PAGES][:].indirect(idx2[:]), h[:, s, :], weight, ALU.mult)

            def fetch(i, cols):
                s = PACK * b + i
                picks = idx3[:, cols.start // 16 : cols.stop // 16]
                nc.vector.tensor_copy(x[:, i, cols], pages[s % PAGES][:].indirect(picks))
                nc.scalar.activation(e[:, i, cols], x[:, i, cols], ACT.Tanh)
                nc.scalar.activation(e[:, i, cols], e[:, i, cols], ACT.Exp)

            for i0 in range(0, PACK, PAGES):
                last = b == PASSES2 - 1 and i0 == PACK - PAGES
                for i in range(i0, i0 + PAGES):
                    put(i)
                for cols in halves if last else [slice(0, M)]:
                    for i in range(i0, i0 + PAGES):
                        fetch(i, cols)

            for u, cols in enumerate(halves):
                z = keep.tile([P, HALF, PACK], BF16, name=f"z{b}{u}", align_bytes=64)
                nc.vector.tensor_tensor(
                    z[:].rearrange("p (c n) i -> p c i n", n=2),
                    e[:, :, cols].rearrange("p i (c n) -> p c i n", n=2),
                    gmap_t[:, :, cols].rearrange("p i (c n) -> p c i n", n=2),
                    ALU.mult,
                )
                z_w = keep.tile([P, HALF], U32, name=f"z_w{b}{u}", align_bytes=64)
                z_s = keep.tile([P, HALF], U8, name=f"z_s{b}{u}", align_bytes=64)
                nc.vector.quantize_mx(z_w[:].bitcast(FP8X4), z_s[:], z[:].rearrange("p c i -> p (c i)"))
                for pair in range(SLICES // 2):
                    if b == 0:
                        banks[u, pair] = psum.tile([P, 2, HALF], F32, name=f"y{u}{pair}", tag=f"bank{4 * u + pair}")
                    for j in range(2):
                        nb, ni = divmod(2 * pair + j, PACK)
                        nc.tensor.matmul_mx(
                            banks[u, pair][:, j, :],
                            lhsT=w2_w[b, nb][:, P * ni : P * (ni + 1)].bitcast(FP8X4),
                            lhsT_scale=w2_s[b, nb][:, P * ni : P * (ni + 1)],
                            rhs=z_w[:].bitcast(FP8X4),
                            rhs_scale=z_s[:],
                            start=(b == 0 and j == 0),
                            stop=(b == PASSES2 - 1 and j == 1),
                        )

        for u, cols in enumerate(halves):
            for pair in range(SLICES // 2):
                nb, ni = divmod(2 * pair, PACK)
                rows = x_t[nb][:, ni : ni + 2, cols]
                nc.vector.tensor_tensor(rows, banks[u, pair][:], rows, ALU.add)
                nc.sync.dma_start(by_rows(out)[nb][:, ni : ni + 2, cols], rows)
